import numpy as np
import ml_dtypes


def mxq(x, axis, fmt="e4m3"):
    dtype, down = {"e4m3": (ml_dtypes.float8_e4m3fn, 7), "e5m2": (ml_dtypes.float8_e5m2, 14)}[fmt]
    v = np.moveaxis(np.asarray(x, np.float32).astype(ml_dtypes.bfloat16).astype(np.float64), axis, -1)
    blocks = v.reshape(v.shape[:-1] + (-1, 32))
    amax = np.abs(blocks).max(-1, keepdims=True)
    byte = np.maximum(np.where(amax > 0, np.frexp(amax)[1] - 1 + 127, 0) - down, 1)
    scale = np.exp2(byte - 127.0)
    codes = (blocks / scale).astype(np.float32).astype(dtype).astype(np.float64)
    return np.moveaxis((codes * scale).reshape(v.shape), -1, axis)


WIDE = False


def mx_kscale(k):
    if not WIDE:
        return np.ones(k)
    levels = np.array([10, -10, 5, -5, 0])
    if k % 512:
        return np.exp2(np.random.permutation(np.resize(levels, k // 32))).repeat(32)
    a = np.empty((k // 512, 16))
    for p in range(k // 512):
        a[p, :8] = np.random.permutation(np.resize(levels, 8))
        for g in range(8):
            far = levels[np.abs(levels - a[p, g]) >= 10]
            a[p, g + 8] = far[np.random.randint(len(far))]
    return np.exp2(a.ravel()).repeat(32)


def f64(x):
    return np.asarray(x).astype(np.float64)


def striped(idx):
    return np.tile(idx.reshape(-1, 16).T, (8, 1)).astype(np.uint16)


def unstriped(offs):
    return offs[:16].T.reshape(-1).astype(np.int64)


E2M1 = np.array([0.0, 0.5, 1.0, 1.5, 2.0, 3.0, 4.0, 6.0, -0.0, -0.5, -1.0, -1.5, -2.0, -3.0, -4.0, -6.0])


def pack_weight(w, fmt):
    k, n = w.shape
    w = f64(np.asarray(w, np.float32).astype(ml_dtypes.bfloat16)).reshape(k // 32, 32, n)
    amax = np.abs(w).max(1)
    if fmt == "e4m3":
        byte = np.frexp(amax)[1] - 1 + 127 - 7
    else:
        mant, ex = np.frexp(amax / 6.0)
        byte = np.where(mant > 0.5, ex, ex - 1) + 127
    byte = np.clip(np.where(amax > 0, byte, 1), 1, 254)
    scaled = (w * np.exp2(127.0 - byte)[:, None, :]).reshape(k, n).astype(np.float32)
    by_word = np.ascontiguousarray(scaled.reshape(k // 512, 128, 4, n).transpose(0, 1, 3, 2))
    if fmt == "e4m3":
        words = by_word.astype(ml_dtypes.float8_e4m3fn).view(np.uint8)
    else:
        c = by_word.astype(ml_dtypes.float4_e2m1fn).view(np.uint8) & 0xF
        words = (c[..., 0::2] | (c[..., 1::2] << 4)).reshape(k // 512, 128, 2 * n)
    return np.ascontiguousarray(words), np.ascontiguousarray(byte.astype(np.uint8).reshape(k // 512, 16, n))


def unpack_weight(words, scales, fmt):
    g, _, n = scales.shape
    words = np.ascontiguousarray(words).reshape(g, 128, n, -1)
    if fmt == "e4m3":
        vals = words.view(ml_dtypes.float8_e4m3fn).astype(np.float64)
    else:
        nib = np.empty((g, 128, n, 4), np.uint8)
        nib[..., 0::2] = words & 0xF
        nib[..., 1::2] = words >> 4
        vals = E2M1[nib]
    vals = vals * np.repeat(np.exp2(scales.astype(np.float64) - 127.0), 8, axis=1)[..., None]
    return vals.transpose(0, 1, 3, 2).reshape(g * 512, n)


def gelu(v):
    return 0.5 * v * (1.0 + np.tanh(np.sqrt(2.0 / np.pi) * (v + 0.044715 * v**3)))


K, T, S, H, T2, P = 1024, 4096, 1024, 512, 2048, 1024

def setup_inputs():
    n = np.random.standard_normal
    s = mx_kscale(K)[:, None]
    u = mx_kscale(H)[:, None]
    d = {}
    d["tab_words"], d["tab_scales"] = pack_weight(n((K, T)) * s, "e4m3")
    d["offs"] = striped(np.random.permutation(T)[:S])
    d["w1_words"], d["w1_scales"] = pack_weight(2.0 * n((K, H)) / K ** 0.5 / s, "e2m1")
    d["w2"] = (2.0 * n((K, H)) / K ** 0.5 / s).astype(np.float32)
    d["gain"] = (np.exp(0.3 * n(H)) * u[:, 0]).astype(np.float32)
    d["page0"] = (n((H, T2)) * u).astype(np.float32)
    d["wgs"] = np.exp(0.3 * n((128, S))).astype(np.float32)
    d["offs2"] = striped(np.random.permutation(T2)[:S])
    d["offs3"] = striped(np.random.permutation(T2)[:P])
    d["offs4"] = striped(np.random.permutation(T2)[:P])
    d["reread"] = np.exp(0.4 * n(H)).astype(np.float32)
    d["w3_words"], d["w3_scales"] = pack_weight(n((H, H)) / H ** 0.5 / u, "e4m3")
    d["sister"] = (np.exp(0.3 * n(H)) / u[:, 0]).astype(np.float32)
    return d

def reference(tab_words, tab_scales, offs, w1_words, w1_scales, w2, gain, page0, wgs, offs2, offs3, offs4, reread, w3_words, w3_scales, sister):
    v = unpack_weight(tab_words, tab_scales, "e4m3")[:, unstriped(offs)]
    w1 = unpack_weight(w1_words, w1_scales, "e2m1")
    w3 = unpack_weight(w3_words, w3_scales, "e4m3")
    lead = w1.T @ v
    temper = mxq(f64(w2), 0, "e4m3").T @ v
    h = lead / np.sqrt(1.0 + np.square(temper)) * f64(gain)[:, None]
    page = f64(page0).copy()
    page[:, unstriped(offs2)] = np.tile(f64(wgs), (H // 128, 1)) * h
    x = page[:, unstriped(offs3)] * f64(reread)[:, None]
    y = w3.T @ mxq(x, 0, "e4m3")
    return y - f64(sister)[:, None] * page[:, unstriped(offs4)]

@@ -1,0 +1,210 @@
+from contextlib import ExitStack
+
+import concourse.mybir as mybir
+
+K, T, S, H, T2, PICKS = 1024, 4096, 1024, 512, 2048, 1024
+FLOPS = 2 * (2 * K * H * S + H * H * PICKS)
+
+F32 = mybir.dt.float32
+BF16 = mybir.dt.bfloat16
+I32 = mybir.dt.int32
+U32 = mybir.dt.uint32
+U16 = mybir.dt.uint16
+U8 = mybir.dt.uint8
+FP8X4 = mybir.dt.float8_e4m3fn_x4
+FP4X4 = mybir.dt.float4_e2m1fn_x4
+ALU = mybir.AluOpType
+ACT = mybir.ActivationFunctionType
+
+P = 128
+PACK = 4
+PASSES = K // (P * PACK)
+N = 512
+QUADS = 4
+LIST_COLS = N // 16
+
+
+def tile_list_cask_blend_scores_kernel(tc, tab_words, tab_scales, offs, w1_words, w1_scales, w2, gain, page0,
+                                                wgs, offs2, offs3, offs4, reread, w3_words, w3_scales, sister, out):
+    nc = tc.nc
+    with ExitStack() as ctx:
+        keep = ctx.enter_context(tc.tile_pool(name="keep", bufs=1))
+        ring = ctx.enter_context(tc.tile_pool(name="ring", bufs=2))
+        psum = ctx.enter_context(tc.psum_pool(name="psum", bufs=4))
+
+        def load_list(src, name):
+            lst = keep.tile([P, S // 16], U16, name=name)
+            nc.sync.dma_start(lst[:], src)
+            return lst
+
+        def half(lst, b):
+            return lst[:, b * LIST_COLS:(b + 1) * LIST_COLS]
+
+        w1_sc_raw = keep.tile([P, PASSES, H], U8, name="w1_sc_raw")
+        w3_sc_raw = keep.tile([P, H], U8, name="w3_sc_raw")
+        tab_sc = keep.tile([P, T], U8, name="tab_sc")
+        nc.vector.memset(w1_sc_raw[:].bitcast(I32), 0)
+        nc.vector.memset(tab_sc[32:64].bitcast(I32), 0)
+        nc.vector.memset(tab_sc[64:128].bitcast(I32), 0)
+        nc.vector.memset(w3_sc_raw[:].bitcast(I32), 0)
+
+        idx = load_list(offs, "idx")
+        nc.sync.dma_start(tab_sc[0:32].bitcast(I32), tab_scales.rearrange("a q t -> q a t").bitcast(I32))
+        w1_raw = keep.tile([P, PASSES, 2 * H], U8, name="w1_raw")
+        nc.sync.dma_start(w1_raw[:].bitcast(I32), w1_words.rearrange("a p c -> p a c").bitcast(I32))
+        tab = [keep.tile([P, T], I32, name=f"tab{a}") for a in range(PASSES)]
+        nc.sync.dma_start(tab[0][:], tab_words[0].rearrange("p t i -> p (t i)").bitcast(I32))
+        for q in range(QUADS):
+            nc.sync.dma_start(w1_sc_raw[32 * q:32 * q + 4].bitcast(I32),
+                              w1_scales[:, 4 * q:4 * q + 4, :].rearrange("a r c -> r a c").bitcast(I32))
+        w3_raw = keep.tile([P, H], I32, name="w3_raw", tag="w3_raw", align_bytes=64)
+        nc.gpsimd.dma_start(w3_raw[:], w3_words[0].rearrange("p c i -> p (c i)").bitcast(I32))
+        for q in range(QUADS):
+            nc.gpsimd.dma_start(w3_sc_raw[32 * q:32 * q + 4].bitcast(I32), w3_scales[0, 4 * q:4 * q + 4, :].bitcast(I32))
+        nc.sync.dma_start(tab[1][:], tab_words[1].rearrange("p t i -> p (t i)").bitcast(I32))
+
+        w1_codes = keep.tile([P, PASSES, 2 * H], U8, name="w1_codes", align_bytes=64)
+        for a in range(PASSES):
+            nc.vector.tensor_copy(w1_codes[:, a, :].rearrange("p (t m e) -> p t m e", t=PACK, e=2),
+                                  w1_raw[:, a, :].rearrange("p (m t e) -> p t m e", t=PACK, e=2))
+        v_sc_rows = keep.tile([P, S], U8, name="v_sc_rows")
+        nc.vector.tensor_copy(v_sc_rows[:], tab_sc[:].indirect(idx[:]))
+        v_sc = keep.tile([P, PASSES, S], U8, name="v_sc", align_bytes=64)
+        for q in range(QUADS):
+            nc.sync.dma_start(v_sc[32 * q:32 * q + 4].bitcast(I32), v_sc_rows[8 * q:8 * q + 8].bitcast(I32))
+
+        w2_raw = [keep.tile([P, PACK, H], F32, name=f"w2_raw{a}") for a in range(PASSES)]
+        for a in range(PASSES):
+            nc.sync.dma_start(w2_raw[a][:], w2[a * P * PACK:(a + 1) * P * PACK, :].rearrange("(p i) c -> p i c", i=PACK))
+        gain_sb = keep.tile([P, PACK], F32, name="gain_sb")
+        nc.sync.dma_start(gain_sb[:], gain.rearrange("(p t) -> p t", t=PACK))
+        idx2 = load_list(offs2, "idx2")
+        page = [keep.tile([P, T2], F32, name=f"page{t}") for t in range(PACK)]
+        page_rows = page0.rearrange("(p t) c -> t p c", t=PACK)
+        nc.sync.dma_start(page[0][:], page_rows[0])
+        wgs_rows = wgs.rearrange("(u t) j -> u t j", t=PACK)
+        wgs_first = [keep.tile([P, N], F32, name=f"wgs_first{b}") for b in range(S // N)]
+        for b in range(S // N):
+            for q in (0, 2, 1, 3):
+                nc.sync.dma_start(wgs_first[b][32 * q:32 * q + 32], wgs_rows[:, 0, b * N:(b + 1) * N])
+        idx3 = load_list(offs3, "idx3")
+        reread_sb = keep.tile([P, PACK], F32, name="reread_sb")
+        nc.sync.dma_start(reread_sb[:], reread.rearrange("(p t) -> p t", t=PACK))
+        idx4 = load_list(offs4, "idx4")
+        nc.sync.dma_start(page[1][:], page_rows[1])
+        wgs_rest = keep.tile([P, PACK - 1, S], F32, name="wgs_rest", tag="late")
+        for q in (0, 2, 1, 3):
+            nc.sync.dma_start(wgs_rest[32 * q:32 * q + 32], wgs_rows[:, 1:, :])
+        for t in range(2, PACK):
+            nc.sync.dma_start(page[t][:], page_rows[t])
+        sister_sb = keep.tile([P, PACK], F32, name="sister_sb")
+        nc.sync.dma_start(sister_sb[:], sister.rearrange("(p t) -> p t", t=PACK))
+
+        warm = keep.tile([P, 1], F32, name="warm")
+        warm_in = keep.tile([P, 1], F32, name="warm_in")
+        nc.gpsimd.memset(warm_in[:], 0.0)
+        nc.scalar.activation(warm[:], warm_in[:], ACT.Abs_reciprocal_sqrt, bias=1.0)
+
+        v = [keep.tile([P, S], U32, name=f"v{a}", align_bytes=64) for a in range(PASSES)]
+        nc.vector.tensor_copy(v[0][:], tab[0][:].bitcast(U32).indirect(idx[:]))
+        w1_sc = keep.tile([P, PASSES, H], U8, name="w1_sc", align_bytes=64)
+        nc.vector.tensor_copy(w1_sc[:].rearrange("p a (t m) -> p a t m", t=PACK),
+                              w1_sc_raw[:].rearrange("p a (m t) -> p a t m", t=PACK))
+        nc.vector.tensor_copy(v[1][:], tab[1][:].bitcast(U32).indirect(idx[:]))
+
+        w2_codes = [keep.tile([P, H], U32, name=f"w2_codes{a}", align_bytes=64) for a in range(PASSES)]
+        w2_sc = [keep.tile([P, H], U8, name=f"w2_sc{a}", align_bytes=64) for a in range(PASSES)]
+
+        def group_w2(copy, a, t0, t1, tag):
+            grouped = keep.tile([P, t1 - t0, P, PACK], BF16, name=f"w2_bf{a}{t0}", tag=tag, align_bytes=64)
+            copy(grouped[:].rearrange("p t m i -> p m i t"),
+                 w2_raw[a][:].rearrange("p i (m t) -> p m i t", t=PACK)[:, :, :, t0:t1])
+            return grouped
+
+        def quantise_w2(a, t0, t1, grouped):
+            nc.vector.quantize_mx(out=w2_codes[a][:, P * t0:P * t1].bitcast(FP8X4), scales=w2_sc[a][:, P * t0:P * t1],
+                                  in_=grouped.rearrange("p t m i -> p (t m i)"))
+
+        quantise_w2(0, 0, PACK, group_w2(nc.vector.tensor_copy, 0, 0, PACK, "w2_bf0")[:])
+        quantise_w2(1, 0, 1, group_w2(nc.vector.tensor_copy, 1, 0, 1, "w2_bf1")[:])
+
+        w3_codes = keep.tile([P, H], I32, name="w3_codes", tag="w2_bf1", align_bytes=64)
+        w3_sc = keep.tile([P, H], U8, name="w3_sc", tag="w3_raw", align_bytes=64)
+        nc.vector.tensor_copy(w3_codes[:].rearrange("p (t m) -> p t m", t=PACK),
+                              w3_raw[:].rearrange("p (m t) -> p t m", t=PACK))
+        nc.vector.tensor_copy(w3_sc[:].rearrange("p (t m) -> p t m", t=PACK),
+                              w3_sc_raw[:].rearrange("p (m t) -> p t m", t=PACK))
+
+        neg_sister = keep.tile([P, PACK], F32, name="neg_sister")
+        nc.scalar.mul(neg_sister[:], sister_sb[:], -1.0)
+
+        x_planes = keep.tile([P, PACK, PICKS], BF16, name="x_planes")
+        sis0 = keep.tile([P, PICKS], F32, name="sis0")
+        for t in range(PACK):
+            for b in range(S // N):
+                cols = slice(b * N, (b + 1) * N)
+                wgs_tb = wgs_first[b][:] if t == 0 else wgs_rest[:, t - 1, cols]
+                lead = psum.tile([P, N], F32, name="lead", tag="acc0")
+                for a in range(PASSES):
+                    nc.tensor.matmul_mx(out=lead[:], lhsT=w1_codes[:, a, 2 * P * t:2 * P * (t + 1)].bitcast(FP4X4),
+                                        lhsT_scale=w1_sc[:, a, P * t:P * (t + 1)],
+                                        rhs=v[a][:, cols].bitcast(FP8X4), rhs_scale=v_sc[:, a, cols],
+                                        start=(a == 0), stop=(a == PASSES - 1))
+                width = N // 2 if (t, b) == (0, 0) else N
+                for c0 in range(0, N, width):
+                    part = slice(c0, c0 + width)
+                    entries = slice(b * N + c0, b * N + c0 + width)
+                    temper = psum.tile([P, width], F32, name="temper", tag="acc1")
+                    for a in range(PASSES):
+                        nc.tensor.matmul_mx(out=temper[:], lhsT=w2_codes[a][:, P * t:P * (t + 1)].bitcast(FP8X4),
+                                            lhsT_scale=w2_sc[a][:, P * t:P * (t + 1)],
+                                            rhs=v[a][:, entries].bitcast(FP8X4), rhs_scale=v_sc[:, a, entries],
+                                            start=(a == 0), stop=(a == PASSES - 1))
+                    if (t, b, c0) == (0, 0, N // 2):
+                        sq = keep.tile([P, width], F32, name="sq_first", tag="after_first", align_bytes=64)
+                    else:
+                        sq = ring.tile([P, width], F32, name="sq")
+                    nc.scalar.activation(sq[:], temper[:], ACT.Square)
+                    damp = ring.tile([P, width], F32, name="damp", bufs=4)
+                    nc.scalar.activation(damp[:], sq[:], ACT.Abs_reciprocal_sqrt, bias=1.0)
+                    if (t, b) == (0, 1):
+                        h = keep.tile([P, width], F32, name="h_second", tag="after_first", align_bytes=64)
+                    else:
+                        h = ring.tile([P, width], F32, name="h")
+                    nc.vector.scalar_tensor_tensor(h[:], lead[:, part], gain_sb[:, t:t + 1], damp[:], ALU.mult, ALU.mult)
+                    nc.vector.tensor_tensor(page[t][:].indirect(idx2[:, entries.start // 16:entries.stop // 16]),
+                                            h[:], wgs_tb[:, part], ALU.mult)
+                if (t, b) == (0, 0):
+                    rest = group_w2(nc.scalar.copy, 1, 1, PACK, "after_first")
+                    quantise_w2(1, 1, 2, rest[:, 0:1])
+                    quantise_w2(1, 2, PACK, rest[:, 1:])
+            for b in range(PICKS // N):
+                picked = ring.tile([P, N], F32, name="picked")
+                nc.vector.tensor_copy(picked[:], page[t][:].indirect(half(idx3, b)))
+                nc.scalar.activation(x_planes[:, t, b * N:(b + 1) * N], picked[:], ACT.Copy, scale=reread_sb[:, t:t + 1])
+            if t == 0:
+                nc.vector.tensor_copy(sis0[:], page[0][:].indirect(idx4[:]))
+
+        sis_rest = keep.tile([P, PACK - 1, PICKS], F32, name="sis_rest", tag="late")
+        for t in range(1, PACK):
+            nc.vector.tensor_copy(sis_rest[:, t - 1, :], page[t][:].indirect(idx4[:]))
+
+        out_rows = out.rearrange("(p t) j -> t p j", t=PACK)
+        for b in range(PICKS // N):
+            cols = slice(b * N, (b + 1) * N)
+            x_grouped = ring.tile([P, N, PACK], BF16, name="x_grouped", align_bytes=64)
+            nc.scalar.copy(x_grouped[:].rearrange("p (c i) t -> p c t i", i=4),
+                           x_planes[:, :, cols].rearrange("p t (c i) -> p c t i", i=4))
+            x_codes = ring.tile([P, N], U32, name="x_codes", align_bytes=64)
+            x_sc = ring.tile([P, N], U8, name="x_sc", align_bytes=64)
+            nc.vector.quantize_mx(out=x_codes[:].bitcast(FP8X4), scales=x_sc[:],
+                                  in_=x_grouped[:].rearrange("p j t -> p (j t)"))
+            for t in range(PACK):
+                y = psum.tile([P, N], F32, name="y", tag=f"acc{b}")
+                nc.tensor.matmul_mx(out=y[:], lhsT=w3_codes[:, P * t:P * (t + 1)].bitcast(FP8X4),
+                                    lhsT_scale=w3_sc[:, P * t:P * (t + 1)],
+                                    rhs=x_codes[:].bitcast(FP8X4), rhs_scale=x_sc[:], start=True, stop=True)
+                sis_t = sis0[:] if t == 0 else sis_rest[:, t - 1, :]
+                res = ring.tile([P, N], F32, name="res", bufs=4)
+                nc.vector.scalar_tensor_tensor(res[:], sis_t[:, cols], neg_sister[:, t:t + 1], y[:], ALU.mult, ALU.add)
+                nc.sync.dma_start(out_rows[t][:, cols], res[:])

@@ -1,6 +1,7 @@
 from contextlib import ExitStack
 
 import concourse.mybir as mybir
+from concourse.masks import make_identity
 
 K, T, S, H, T2, PICKS = 1024, 4096, 1024, 512, 2048, 1024
 FLOPS = 2 * (2 * K * H * S + H * H * PICKS)
@@ -19,9 +20,10 @@ ACT = mybir.ActivationFunctionType
 P = 128
 PACK = 4
 PASSES = K // (P * PACK)
+SLICES = H // P
 N = 512
 QUADS = 4
-LIST_COLS = N // 16
+BLOCKS = N // P
 
 
 def tile_list_cask_blend_scores_kernel(tc, tab_words, tab_scales, offs, w1_words, w1_scales, w2, gain, page0,
@@ -30,181 +32,237 @@ def tile_list_cask_blend_scores_kernel(tc, tab_words, tab_scales, offs, w1_words
     with ExitStack() as ctx:
         keep = ctx.enter_context(tc.tile_pool(name="keep", bufs=1))
         ring = ctx.enter_context(tc.tile_pool(name="ring", bufs=2))
-        psum = ctx.enter_context(tc.psum_pool(name="psum", bufs=4))
+        psum = ctx.enter_context(tc.psum_pool(name="psum", bufs=2))
+        halves = [slice(b * N, (b + 1) * N) for b in range(S // N)]
 
         def load_list(src, name):
             lst = keep.tile([P, S // 16], U16, name=name)
             nc.sync.dma_start(lst[:], src)
             return lst
 
-        def half(lst, b):
-            return lst[:, b * LIST_COLS:(b + 1) * LIST_COLS]
+        def load_channel_vector(src, name):
+            vec = keep.tile([P, SLICES], F32, name=name)
+            with nc.allow_non_contiguous_dma(reason="one value for each channel and partition"):
+                nc.sync.dma_start(vec[:], src.rearrange("(c p) -> p c", p=P))
+            return vec
 
-        w1_sc_raw = keep.tile([P, PASSES, H], U8, name="w1_sc_raw")
-        w3_sc_raw = keep.tile([P, H], U8, name="w3_sc_raw")
+        def load_w2(c0, c1):
+            raw = keep.tile([P, PASSES, PACK, (c1 - c0) * P], F32, name=f"w2_raw{c0}")
+            for a in range(PASSES):
+                rows = w2[a * P * PACK:(a + 1) * P * PACK, c0 * P:c1 * P]
+                nc.sync.dma_start(raw[:, a], rows.rearrange("(p i) m -> p i m", i=PACK))
+            return [raw[:, :, :, (c - c0) * P:(c - c0 + 1) * P] for c in range(c0, c1)]
+
+        def columns(lst, entries):
+            return lst[:, entries.start // 16:entries.stop // 16]
+
         tab_sc = keep.tile([P, T], U8, name="tab_sc")
-        nc.vector.memset(w1_sc_raw[:].bitcast(I32), 0)
         nc.vector.memset(tab_sc[32:64].bitcast(I32), 0)
         nc.vector.memset(tab_sc[64:128].bitcast(I32), 0)
-        nc.vector.memset(w3_sc_raw[:].bitcast(I32), 0)
 
         idx = load_list(offs, "idx")
         nc.sync.dma_start(tab_sc[0:32].bitcast(I32), tab_scales.rearrange("a q t -> q a t").bitcast(I32))
-        w1_raw = keep.tile([P, PASSES, 2 * H], U8, name="w1_raw")
-        nc.sync.dma_start(w1_raw[:].bitcast(I32), w1_words.rearrange("a p c -> p a c").bitcast(I32))
+        w1_codes = keep.tile([P, PASSES, 2 * H], U8, name="w1_codes", align_bytes=64)
+        nc.sync.dma_start(w1_codes[:].bitcast(I32), w1_words.rearrange("a p c -> p a c").bitcast(I32))
         tab = [keep.tile([P, T], I32, name=f"tab{a}") for a in range(PASSES)]
         nc.sync.dma_start(tab[0][:], tab_words[0].rearrange("p t i -> p (t i)").bitcast(I32))
+        w1_sc = keep.tile([P, PASSES, H], U8, name="w1_sc", align_bytes=64)
         for q in range(QUADS):
-            nc.sync.dma_start(w1_sc_raw[32 * q:32 * q + 4].bitcast(I32),
+            nc.sync.dma_start(w1_sc[32 * q:32 * q + 4].bitcast(I32),
                               w1_scales[:, 4 * q:4 * q + 4, :].rearrange("a r c -> r a c").bitcast(I32))
-        w3_raw = keep.tile([P, H], I32, name="w3_raw", tag="w3_raw", align_bytes=64)
-        nc.gpsimd.dma_start(w3_raw[:], w3_words[0].rearrange("p c i -> p (c i)").bitcast(I32))
-        for q in range(QUADS):
-            nc.gpsimd.dma_start(w3_sc_raw[32 * q:32 * q + 4].bitcast(I32), w3_scales[0, 4 * q:4 * q + 4, :].bitcast(I32))
+        w2_raw = load_w2(0, 1)
         nc.sync.dma_start(tab[1][:], tab_words[1].rearrange("p t i -> p (t i)").bitcast(I32))
 
-        w1_codes = keep.tile([P, PASSES, 2 * H], U8, name="w1_codes", align_bytes=64)
-        for a in range(PASSES):
-            nc.vector.tensor_copy(w1_codes[:, a, :].rearrange("p (t m e) -> p t m e", t=PACK, e=2),
-                                  w1_raw[:, a, :].rearrange("p (m t e) -> p t m e", t=PACK, e=2))
         v_sc_rows = keep.tile([P, S], U8, name="v_sc_rows")
         nc.vector.tensor_copy(v_sc_rows[:], tab_sc[:].indirect(idx[:]))
         v_sc = keep.tile([P, PASSES, S], U8, name="v_sc", align_bytes=64)
         for q in range(QUADS):
             nc.sync.dma_start(v_sc[32 * q:32 * q + 4].bitcast(I32), v_sc_rows[8 * q:8 * q + 8].bitcast(I32))
 
-        w2_raw = [keep.tile([P, PACK, H], F32, name=f"w2_raw{a}") for a in range(PASSES)]
-        for a in range(PASSES):
-            nc.sync.dma_start(w2_raw[a][:], w2[a * P * PACK:(a + 1) * P * PACK, :].rearrange("(p i) c -> p i c", i=PACK))
-        gain_sb = keep.tile([P, PACK], F32, name="gain_sb")
-        nc.sync.dma_start(gain_sb[:], gain.rearrange("(p t) -> p t", t=PACK))
+        gain_sb = load_channel_vector(gain, "gain_sb")
         idx2 = load_list(offs2, "idx2")
-        page = [keep.tile([P, T2], F32, name=f"page{t}") for t in range(PACK)]
-        page_rows = page0.rearrange("(p t) c -> t p c", t=PACK)
-        nc.sync.dma_start(page[0][:], page_rows[0])
-        wgs_rows = wgs.rearrange("(u t) j -> u t j", t=PACK)
-        wgs_first = [keep.tile([P, N], F32, name=f"wgs_first{b}") for b in range(S // N)]
-        for b in range(S // N):
-            for q in (0, 2, 1, 3):
-                nc.sync.dma_start(wgs_first[b][32 * q:32 * q + 32], wgs_rows[:, 0, b * N:(b + 1) * N])
+        page = [keep.tile([P, T2], F32, name=f"page{c}") for c in range(SLICES)]
+        nc.sync.dma_start(page[0][:], page0[0:P, :])
+        wgs_sb = keep.tile([P, S], F32, name="wgs_sb")
+        first, later = slice(0, N // 2), slice(N // 2, S)
+        nc.sync.dma_start(wgs_sb[:, first], wgs[:, first])
+        w2_raw = w2_raw + load_w2(1, 2)
+        nc.sync.dma_start(wgs_sb[:, later], wgs[:, later])
+        w2_raw = w2_raw + load_w2(2, SLICES)
         idx3 = load_list(offs3, "idx3")
-        reread_sb = keep.tile([P, PACK], F32, name="reread_sb")
-        nc.sync.dma_start(reread_sb[:], reread.rearrange("(p t) -> p t", t=PACK))
+        reread_sb = load_channel_vector(reread, "reread_sb")
+        for c in range(1, SLICES):
+            nc.sync.dma_start(page[c][:], page0[c * P:(c + 1) * P, :])
         idx4 = load_list(offs4, "idx4")
-        nc.sync.dma_start(page[1][:], page_rows[1])
-        wgs_rest = keep.tile([P, PACK - 1, S], F32, name="wgs_rest", tag="late")
-        for q in (0, 2, 1, 3):
-            nc.sync.dma_start(wgs_rest[32 * q:32 * q + 32], wgs_rows[:, 1:, :])
-        for t in range(2, PACK):
-            nc.sync.dma_start(page[t][:], page_rows[t])
-        sister_sb = keep.tile([P, PACK], F32, name="sister_sb")
-        nc.sync.dma_start(sister_sb[:], sister.rearrange("(p t) -> p t", t=PACK))
+        sister_sb = load_channel_vector(sister, "sister_sb")
+        w3_codes = keep.tile([P, H], I32, name="w3_codes", align_bytes=64)
+        nc.sync.dma_start(w3_codes[:], w3_words[0].rearrange("p c i -> p (c i)").bitcast(I32))
+        w3_sc = keep.tile([P, H], U8, name="w3_sc", align_bytes=64)
+        for q in range(QUADS):
+            nc.sync.dma_start(w3_sc[32 * q:32 * q + 4].bitcast(I32), w3_scales[0, 4 * q:4 * q + 4, :].bitcast(I32))
 
         warm = keep.tile([P, 1], F32, name="warm")
         warm_in = keep.tile([P, 1], F32, name="warm_in")
         nc.gpsimd.memset(warm_in[:], 0.0)
         nc.scalar.activation(warm[:], warm_in[:], ACT.Abs_reciprocal_sqrt, bias=1.0)
+        ident_bf = keep.tile([P, P], BF16, name="ident_bf")
+        make_identity(nc, ident_bf[:])
+        ident_f32 = keep.tile([P, P], F32, name="ident_f32")
+        make_identity(nc, ident_f32[:])
 
-        v = [keep.tile([P, S], U32, name=f"v{a}", align_bytes=64) for a in range(PASSES)]
-        nc.vector.tensor_copy(v[0][:], tab[0][:].bitcast(U32).indirect(idx[:]))
-        w1_sc = keep.tile([P, PASSES, H], U8, name="w1_sc", align_bytes=64)
-        nc.vector.tensor_copy(w1_sc[:].rearrange("p a (t m) -> p a t m", t=PACK),
-                              w1_sc_raw[:].rearrange("p a (m t) -> p a t m", t=PACK))
-        nc.vector.tensor_copy(v[1][:], tab[1][:].bitcast(U32).indirect(idx[:]))
+        w2_codes = [keep.tile([P, PASSES, P], U32, name=f"w2_codes{c}", align_bytes=64) for c in range(SLICES)]
+        w2_sc = [keep.tile([P, PASSES, P], U8, name=f"w2_sc{c}", align_bytes=64) for c in range(SLICES)]
 
-        w2_codes = [keep.tile([P, H], U32, name=f"w2_codes{a}", align_bytes=64) for a in range(PASSES)]
-        w2_sc = [keep.tile([P, H], U8, name=f"w2_sc{a}", align_bytes=64) for a in range(PASSES)]
+        def quantise_w2(c, copy):
+            grouped = keep.tile([P, PASSES, P, PACK], BF16, name=f"w2_bf{c}", tag=f"chain{c}", align_bytes=64)
+            for a in range(PASSES):
+                copy(grouped[:, a].rearrange("p (m e) i -> p m i e", e=4),
+                     w2_raw[c][:, a].rearrange("p i (m e) -> p m i e", e=4))
+            nc.vector.quantize_mx(out=w2_codes[c][:].rearrange("p a m -> p (a m)").bitcast(FP8X4),
+                                  scales=w2_sc[c][:].rearrange("p a m -> p (a m)"),
+                                  in_=grouped[:].rearrange("p a m i -> p (a m i)"))
 
-        def group_w2(copy, a, t0, t1, tag):
-            grouped = keep.tile([P, t1 - t0, P, PACK], BF16, name=f"w2_bf{a}{t0}", tag=tag, align_bytes=64)
-            copy(grouped[:].rearrange("p t m i -> p m i t"),
-                 w2_raw[a][:].rearrange("p i (m t) -> p m i t", t=PACK)[:, :, :, t0:t1])
-            return grouped
+        v = [[keep.tile([P, N], U32, name=f"v{a}{b}", align_bytes=64) for b in range(S // N)] for a in range(PASSES)]
+        for b, entries in enumerate(halves):
+            nc.vector.tensor_copy(v[0][b][:], tab[0][:].bitcast(U32).indirect(columns(idx, entries)))
+        quantise_w2(0, nc.vector.tensor_copy)
+        for b, entries in enumerate(halves):
+            nc.vector.tensor_copy(v[1][b][:], tab[1][:].bitcast(U32).indirect(columns(idx, entries)))
 
-        def quantise_w2(a, t0, t1, grouped):
-            nc.vector.quantize_mx(out=w2_codes[a][:, P * t0:P * t1].bitcast(FP8X4), scales=w2_sc[a][:, P * t0:P * t1],
-                                  in_=grouped.rearrange("p t m i -> p (t m i)"))
-
-        quantise_w2(0, 0, PACK, group_w2(nc.vector.tensor_copy, 0, 0, PACK, "w2_bf0")[:])
-        quantise_w2(1, 0, 1, group_w2(nc.vector.tensor_copy, 1, 0, 1, "w2_bf1")[:])
-
-        w3_codes = keep.tile([P, H], I32, name="w3_codes", tag="w2_bf1", align_bytes=64)
-        w3_sc = keep.tile([P, H], U8, name="w3_sc", tag="w3_raw", align_bytes=64)
-        nc.vector.tensor_copy(w3_codes[:].rearrange("p (t m) -> p t m", t=PACK),
-                              w3_raw[:].rearrange("p (m t) -> p t m", t=PACK))
-        nc.vector.tensor_copy(w3_sc[:].rearrange("p (t m) -> p t m", t=PACK),
-                              w3_sc_raw[:].rearrange("p (m t) -> p t m", t=PACK))
-
-        neg_sister = keep.tile([P, PACK], F32, name="neg_sister")
+        neg_sister = keep.tile([P, SLICES], F32, name="neg_sister")
         nc.scalar.mul(neg_sister[:], sister_sb[:], -1.0)
 
-        x_planes = keep.tile([P, PACK, PICKS], BF16, name="x_planes")
-        sis0 = keep.tile([P, PICKS], F32, name="sis0")
-        for t in range(PACK):
-            for b in range(S // N):
-                cols = slice(b * N, (b + 1) * N)
-                wgs_tb = wgs_first[b][:] if t == 0 else wgs_rest[:, t - 1, cols]
-                lead = psum.tile([P, N], F32, name="lead", tag="acc0")
-                for a in range(PASSES):
-                    nc.tensor.matmul_mx(out=lead[:], lhsT=w1_codes[:, a, 2 * P * t:2 * P * (t + 1)].bitcast(FP4X4),
-                                        lhsT_scale=w1_sc[:, a, P * t:P * (t + 1)],
-                                        rhs=v[a][:, cols].bitcast(FP8X4), rhs_scale=v_sc[:, a, cols],
-                                        start=(a == 0), stop=(a == PASSES - 1))
-                width = N // 2 if (t, b) == (0, 0) else N
-                for c0 in range(0, N, width):
-                    part = slice(c0, c0 + width)
-                    entries = slice(b * N + c0, b * N + c0 + width)
-                    temper = psum.tile([P, width], F32, name="temper", tag="acc1")
-                    for a in range(PASSES):
-                        nc.tensor.matmul_mx(out=temper[:], lhsT=w2_codes[a][:, P * t:P * (t + 1)].bitcast(FP8X4),
-                                            lhsT_scale=w2_sc[a][:, P * t:P * (t + 1)],
-                                            rhs=v[a][:, entries].bitcast(FP8X4), rhs_scale=v_sc[:, a, entries],
-                                            start=(a == 0), stop=(a == PASSES - 1))
-                    if (t, b, c0) == (0, 0, N // 2):
-                        sq = keep.tile([P, width], F32, name="sq_first", tag="after_first", align_bytes=64)
-                    else:
-                        sq = ring.tile([P, width], F32, name="sq")
-                    nc.scalar.activation(sq[:], temper[:], ACT.Square)
-                    damp = ring.tile([P, width], F32, name="damp", bufs=4)
-                    nc.scalar.activation(damp[:], sq[:], ACT.Abs_reciprocal_sqrt, bias=1.0)
-                    if (t, b) == (0, 1):
-                        h = keep.tile([P, width], F32, name="h_second", tag="after_first", align_bytes=64)
-                    else:
-                        h = ring.tile([P, width], F32, name="h")
-                    nc.vector.scalar_tensor_tensor(h[:], lead[:, part], gain_sb[:, t:t + 1], damp[:], ALU.mult, ALU.mult)
-                    nc.vector.tensor_tensor(page[t][:].indirect(idx2[:, entries.start // 16:entries.stop // 16]),
-                                            h[:], wgs_tb[:, part], ALU.mult)
-                if (t, b) == (0, 0):
-                    rest = group_w2(nc.scalar.copy, 1, 1, PACK, "after_first")
-                    quantise_w2(1, 1, 2, rest[:, 0:1])
-                    quantise_w2(1, 2, PACK, rest[:, 1:])
-            for b in range(PICKS // N):
-                picked = ring.tile([P, N], F32, name="picked")
-                nc.vector.tensor_copy(picked[:], page[t][:].indirect(half(idx3, b)))
-                nc.scalar.activation(x_planes[:, t, b * N:(b + 1) * N], picked[:], ACT.Copy, scale=reread_sb[:, t:t + 1])
-            if t == 0:
-                nc.vector.tensor_copy(sis0[:], page[0][:].indirect(idx4[:]))
+        def accumulate(acc, codes, scales, entries):
+            b, c0 = divmod(entries.start, N)
+            part = slice(c0, c0 + entries.stop - entries.start)
+            for a in range(PASSES):
+                nc.tensor.matmul_mx(out=acc, lhsT=codes[a], lhsT_scale=scales[a],
+                                    rhs=v[a][b][:, part].bitcast(FP8X4), rhs_scale=v_sc[:, a, entries],
+                                    start=(a == 0), stop=(a == PASSES - 1))
 
-        sis_rest = keep.tile([P, PACK - 1, PICKS], F32, name="sis_rest", tag="late")
-        for t in range(1, PACK):
-            nc.vector.tensor_copy(sis_rest[:, t - 1, :], page[t][:].indirect(idx4[:]))
+        def lead_of(c, entries):
+            lead = psum.tile([P, N], F32, name="lead", tag="acc0")
+            accumulate(lead[:], [w1_codes[:, a, 2 * P * c:2 * P * (c + 1)].bitcast(FP4X4) for a in range(PASSES)],
+                       [w1_sc[:, a, P * c:P * (c + 1)] for a in range(PASSES)], entries)
+            return lead
 
-        out_rows = out.rearrange("(p t) j -> t p j", t=PACK)
+        def damp_of(c, entries, damp):
+            width = entries.stop - entries.start
+            temper = psum.tile([P, width], F32, name="temper", tag="acc1")
+            accumulate(temper[:], [w2_codes[c][:, a].bitcast(FP8X4) for a in range(PASSES)],
+                       [w2_sc[c][:, a] for a in range(PASSES)], entries)
+            sq = ring.tile([P, width], F32, name="sq")
+            nc.scalar.activation(sq[:], temper[:], ACT.Square)
+            nc.scalar.activation(damp, sq[:], ACT.Abs_reciprocal_sqrt, bias=1.0)
+
+        x_rows = [keep.tile([P, BLOCKS, H], BF16, name=f"x_rows{b}") for b in range(PICKS // N)]
+
+        def reread_casks(c, entries, picked):
+            nc.vector.tensor_copy(picked, page[c][:].indirect(columns(idx3, entries)))
+            for e0 in range(0, entries.stop - entries.start, N):
+                x_c = ring.tile([P, N], BF16, name="x_c")
+                nc.scalar.activation(x_c[:], picked[:, e0:e0 + N], ACT.Copy, scale=reread_sb[:, c:c + 1])
+                turned = psum.tile([P, BLOCKS, P], BF16, name="turned", tag="turn", bufs=4)
+                for jb in range(BLOCKS):
+                    nc.tensor.transpose(turned[:, jb, :], x_c[:, jb * P:(jb + 1) * P], ident_bf[:])
+                nc.scalar.copy(x_rows[(entries.start + e0) // N][:, :, c * P:(c + 1) * P], turned[:])
+
+        def first_damp(entries):
+            damp = ring.tile([P, entries.stop - entries.start], F32, name="damp_first", bufs=3)
+            damp_of(0, entries, damp[:])
+            return damp
+
+        def features(h, lead, damp):
+            nc.vector.scalar_tensor_tensor(h, lead, gain_sb[:, 0:1], damp[:], ALU.mult, ALU.mult)
+
+        def scatter(c, entries, values, weights):
+            nc.vector.tensor_tensor(page[c][:].indirect(columns(idx2, entries)), values, weights, ALU.mult)
+
+        second = slice(N // 2, N)
+        damps = [first_damp(first)]
+        leads = [lead_of(0, halves[0])]
+        damps.append(first_damp(second))
+        damps.append(first_damp(halves[1]))
+        leads.append(lead_of(0, halves[1]))
+        h_first = keep.tile([P, N // 2], F32, name="h_first")
+        features(h_first[:], leads[0][:, first], damps[0])
+        scatter(0, first, h_first[:], wgs_sb[:, first])
+        quantise_w2(1, nc.scalar.copy)
+        h_later = keep.tile([P, S - N // 2], F32, name="h_later", tag="chain1", align_bytes=64)
+        features(h_later[:, 0:N // 2], leads[0][:, second], damps[1])
+        features(h_later[:, N // 2:], leads[1][:], damps[2])
+        scatter(0, later, h_later[:], wgs_sb[:, later])
+
+        damp = {c: keep.tile([P, S], F32, name=f"damp{c}") for c in range(1, SLICES)}
+        gained = {c: keep.tile([P, S], F32, name=f"gained{c}", tag=f"gained{c}") for c in range(1, SLICES)}
+
+        def factors(c):
+            for entries in halves:
+                damp_of(c, entries, damp[c][:, entries])
+            for entries in halves:
+                lead = lead_of(c, entries)
+                nc.scalar.activation(gained[c][:, entries], lead[:], ACT.Copy, scale=gain_sb[:, c:c + 1])
+
+        quantise_w2(2, nc.scalar.copy)
+        factors(1)
+        quantise_w2(3, nc.scalar.copy)
+        factors(2)
+        picked = keep.tile([P, PICKS], F32, name="picked0", tag="chain2", align_bytes=64)
+        reread_casks(0, slice(0, PICKS), picked[:])
+        factors(3)
+        for c in range(1, SLICES):
+            weight = keep.tile([P, S], F32, name=f"weight{c}", tag=f"chain{c}" if c > 1 else "weight1", align_bytes=64)
+            nc.gpsimd.tensor_tensor(weight[:], damp[c][:], wgs_sb[:], ALU.mult)
+            scatter(c, slice(0, S), gained[c][:], weight[:])
+            if c < SLICES - 1:
+                picked = keep.tile([P, PICKS], F32, name=f"picked{c}", tag=f"chain{c + 2}", align_bytes=64)
+                reread_casks(c, slice(0, PICKS), picked[:])
+            else:
+                for entries in halves:
+                    picked = ring.tile([P, N], F32, name="picked_last")
+                    reread_casks(c, entries, picked[:])
+
+        sis = [keep.tile([P, PICKS], F32, name="sis0", tag="gained3"),
+               keep.tile([P, PICKS], F32, name="sis1", tag="chain3", align_bytes=64)]
+        for c in range(2):
+            nc.vector.tensor_copy(sis[c][:], page[c][:].indirect(idx4[:]))
+
+        x_codes = [keep.tile([P, N], U32, name=f"x_codes{b}", align_bytes=64) for b in range(PICKS // N)]
+        x_sc = [keep.tile([P, N], U8, name=f"x_sc{b}", align_bytes=64) for b in range(PICKS // N)]
         for b in range(PICKS // N):
-            cols = slice(b * N, (b + 1) * N)
-            x_grouped = ring.tile([P, N, PACK], BF16, name="x_grouped", align_bytes=64)
-            nc.scalar.copy(x_grouped[:].rearrange("p (c i) t -> p c t i", i=4),
-                           x_planes[:, :, cols].rearrange("p t (c i) -> p c t i", i=4))
-            x_codes = ring.tile([P, N], U32, name="x_codes", align_bytes=64)
-            x_sc = ring.tile([P, N], U8, name="x_sc", align_bytes=64)
-            nc.vector.quantize_mx(out=x_codes[:].bitcast(FP8X4), scales=x_sc[:],
+            x_grouped = keep.tile([P, N, PACK], BF16, name=f"x_grouped{b}", tag=f"x_grouped{b}", align_bytes=64)
+            words = x_rows[b][:].bitcast(F32)
+            for j0 in range(0, BLOCKS, 2):
+                back = psum.tile([P, 2, 2, P], F32, name="back", tag="turn", bufs=4)
+                for jb in range(2):
+                    for u in range(2):
+                        nc.tensor.transpose(back[:, jb, u, :], words[:, j0 + jb, u::2], ident_f32[:])
+                nc.scalar.copy(x_grouped[:, j0 * P:(j0 + 2) * P, :].bitcast(F32).rearrange("p (jb j) u -> p jb j u", jb=2),
+                               back[:].rearrange("p jb u j -> p jb j u"))
+            nc.vector.quantize_mx(out=x_codes[b][:].bitcast(FP8X4), scales=x_sc[b][:],
                                   in_=x_grouped[:].rearrange("p j t -> p (j t)"))
-            for t in range(PACK):
-                y = psum.tile([P, N], F32, name="y", tag=f"acc{b}")
-                nc.tensor.matmul_mx(out=y[:], lhsT=w3_codes[:, P * t:P * (t + 1)].bitcast(FP8X4),
-                                    lhsT_scale=w3_sc[:, P * t:P * (t + 1)],
-                                    rhs=x_codes[:].bitcast(FP8X4), rhs_scale=x_sc[:], start=True, stop=True)
-                sis_t = sis0[:] if t == 0 else sis_rest[:, t - 1, :]
-                res = ring.tile([P, N], F32, name="res", bufs=4)
-                nc.vector.scalar_tensor_tensor(res[:], sis_t[:, cols], neg_sister[:, t:t + 1], y[:], ALU.mult, ALU.add)
-                nc.sync.dma_start(out_rows[t][:, cols], res[:])
+        for c in range(2, SLICES):
+            sis.append(keep.tile([P, PICKS], F32, name=f"sis{c}", tag=f"x_grouped{c - 2}", align_bytes=64))
+            nc.vector.tensor_copy(sis[c][:], page[c][:].indirect(idx4[:]))
+
+        pieces = [(0, 0), (1, 0), (2, 0), (0, 1), (1, 1), (3, 0), (2, 1), (3, 1)]
+        on_gpsimd = 5
+        for i, (c, b) in enumerate(pieces):
+            entries = halves[b]
+            if i < 4:
+                y = psum.tile([P, N], F32, name="y", tag=f"acc{i % 2}")
+            else:
+                y = psum.tile([P, N], F32, name="y", tag="turn", bufs=4)
+            nc.tensor.matmul_mx(out=y[:], lhsT=w3_codes[:, P * c:P * (c + 1)].bitcast(FP8X4),
+                                lhsT_scale=w3_sc[:, P * c:P * (c + 1)],
+                                rhs=x_codes[b][:].bitcast(FP8X4), rhs_scale=x_sc[b][:], start=True, stop=True)
+            res = ring.tile([P, N], F32, name="res", bufs=8)
+            if i < on_gpsimd:
+                y_sb = ring.tile([P, N], F32, name="y_sb", bufs=5)
+                nc.scalar.copy(y_sb[:], y[:])
+                scaled = ring.tile([P, N], F32, name="scaled", bufs=5)
+                nc.scalar.activation(scaled[:], sis[c][:, entries], ACT.Copy, scale=neg_sister[:, c:c + 1])
+                nc.gpsimd.tensor_tensor(res[:], y_sb[:], scaled[:], ALU.add)
+            else:
+                nc.vector.scalar_tensor_tensor(res[:], sis[c][:, entries], neg_sister[:, c:c + 1], y[:], ALU.mult, ALU.add)
+            nc.sync.dma_start(out[c * P:(c + 1) * P, entries], res[:])

@@ -62,8 +62,6 @@ def tile_list_cask_blend_scores_kernel(tc, tab_words, tab_scales, offs, w1_words
 
         idx = load_list(offs, "idx")
         nc.sync.dma_start(tab_sc[0:32].bitcast(I32), tab_scales.rearrange("a q t -> q a t").bitcast(I32))
-        w1_codes = keep.tile([P, PASSES, 2 * H], U8, name="w1_codes", align_bytes=64)
-        nc.sync.dma_start(w1_codes[:].bitcast(I32), w1_words.rearrange("a p c -> p a c").bitcast(I32))
         tab = [keep.tile([P, T], I32, name=f"tab{a}") for a in range(PASSES)]
         nc.sync.dma_start(tab[0][:], tab_words[0].rearrange("p t i -> p (t i)").bitcast(I32))
         w1_sc = keep.tile([P, PASSES, H], U8, name="w1_sc", align_bytes=64)
@@ -79,10 +77,12 @@ def tile_list_cask_blend_scores_kernel(tc, tab_words, tab_scales, offs, w1_words
         for q in range(QUADS):
             nc.sync.dma_start(v_sc[32 * q:32 * q + 4].bitcast(I32), v_sc_rows[8 * q:8 * q + 8].bitcast(I32))
 
-        gain_sb = load_channel_vector(gain, "gain_sb")
-        idx2 = load_list(offs2, "idx2")
+        w1_codes = keep.tile([P, PASSES, 2 * H], U8, name="w1_codes", align_bytes=64)
+        nc.sync.dma_start(w1_codes[:].bitcast(I32), w1_words.rearrange("a p c -> p a c").bitcast(I32))
         page = [keep.tile([P, T2], F32, name=f"page{c}") for c in range(SLICES)]
         nc.sync.dma_start(page[0][:], page0[0:P, :])
+        gain_sb = load_channel_vector(gain, "gain_sb")
+        idx2 = load_list(offs2, "idx2")
         wgs_sb = keep.tile([P, S], F32, name="wgs_sb")
         first, later = slice(0, N // 2), slice(N // 2, S)
         nc.sync.dma_start(wgs_sb[:, first], wgs[:, first])
@@ -172,11 +172,11 @@ def tile_list_cask_blend_scores_kernel(tc, tab_words, tab_scales, offs, w1_words
             damp_of(0, entries, damp[:])
             return damp
 
-        def features(h, lead, damp):
-            nc.vector.scalar_tensor_tensor(h, lead, gain_sb[:, 0:1], damp[:], ALU.mult, ALU.mult)
+        def features(h, lead, factor):
+            nc.vector.scalar_tensor_tensor(h, lead, gain_sb[:, 0:1], factor, ALU.mult, ALU.mult)
 
-        def scatter(c, entries, values, weights):
-            nc.vector.tensor_tensor(page[c][:].indirect(columns(idx2, entries)), values, weights, ALU.mult)
+        def scatter(c, entries, values):
+            nc.vector.tensor_copy(page[c][:].indirect(columns(idx2, entries)), values)
 
         second = slice(N // 2, N)
         damps = [first_damp(first)]
@@ -185,13 +185,16 @@ def tile_list_cask_blend_scores_kernel(tc, tab_words, tab_scales, offs, w1_words
         damps.append(first_damp(halves[1]))
         leads.append(lead_of(0, halves[1]))
         h_first = keep.tile([P, N // 2], F32, name="h_first")
-        features(h_first[:], leads[0][:, first], damps[0])
-        scatter(0, first, h_first[:], wgs_sb[:, first])
+        features(h_first[:], leads[0][:, first], damps[0][:])
+        nc.vector.tensor_tensor(page[0][:].indirect(columns(idx2, first)), h_first[:], wgs_sb[:, first], ALU.mult)
+        weight = keep.tile([P, S - N // 2], F32, name="weight0")
+        nc.gpsimd.tensor_tensor(weight[:, 0:N // 2], damps[1][:], wgs_sb[:, second], ALU.mult)
+        nc.gpsimd.tensor_tensor(weight[:, N // 2:], damps[2][:], wgs_sb[:, halves[1]], ALU.mult)
         quantise_w2(1, nc.scalar.copy)
         h_later = keep.tile([P, S - N // 2], F32, name="h_later", tag="chain1", align_bytes=64)
-        features(h_later[:, 0:N // 2], leads[0][:, second], damps[1])
-        features(h_later[:, N // 2:], leads[1][:], damps[2])
-        scatter(0, later, h_later[:], wgs_sb[:, later])
+        features(h_later[:, 0:N // 2], leads[0][:, second], weight[:, 0:N // 2])
+        features(h_later[:, N // 2:], leads[1][:], weight[:, N // 2:])
+        scatter(0, later, h_later[:])
 
         damp = {c: keep.tile([P, S], F32, name=f"damp{c}") for c in range(1, SLICES)}
         gained = {c: keep.tile([P, S], F32, name=f"gained{c}", tag=f"gained{c}") for c in range(1, SLICES)}
@@ -199,7 +202,6 @@ def tile_list_cask_blend_scores_kernel(tc, tab_words, tab_scales, offs, w1_words
         def factors(c):
             for entries in halves:
                 damp_of(c, entries, damp[c][:, entries])
-            for entries in halves:
                 lead = lead_of(c, entries)
                 nc.scalar.activation(gained[c][:, entries], lead[:], ACT.Copy, scale=gain_sb[:, c:c + 1])
 
@@ -211,9 +213,12 @@ def tile_list_cask_blend_scores_kernel(tc, tab_words, tab_scales, offs, w1_words
         reread_casks(0, slice(0, PICKS), picked[:])
         factors(3)
         for c in range(1, SLICES):
-            weight = keep.tile([P, S], F32, name=f"weight{c}", tag=f"chain{c}" if c > 1 else "weight1", align_bytes=64)
-            nc.gpsimd.tensor_tensor(weight[:], damp[c][:], wgs_sb[:], ALU.mult)
-            scatter(c, slice(0, S), gained[c][:], weight[:])
+            values = keep.tile([P, S], F32, name=f"values{c}", tag=f"values{c}")
+            for entries in halves:
+                weight = ring.tile([P, N], F32, name="weight")
+                nc.gpsimd.tensor_tensor(weight[:], damp[c][:, entries], wgs_sb[:, entries], ALU.mult)
+                nc.gpsimd.tensor_tensor(values[:, entries], gained[c][:, entries], weight[:], ALU.mult)
+            scatter(c, slice(0, S), values[:])
             if c < SLICES - 1:
                 picked = keep.tile([P, PICKS], F32, name=f"picked{c}", tag=f"chain{c + 2}", align_bytes=64)
                 reread_casks(c, slice(0, PICKS), picked[:])
@@ -222,10 +227,10 @@ def tile_list_cask_blend_scores_kernel(tc, tab_words, tab_scales, offs, w1_words
                     picked = ring.tile([P, N], F32, name="picked_last")
                     reread_casks(c, entries, picked[:])
 
-        sis = [keep.tile([P, PICKS], F32, name="sis0", tag="gained3"),
-               keep.tile([P, PICKS], F32, name="sis1", tag="chain3", align_bytes=64)]
+        sis01 = keep.tile([P, 2, PICKS], F32, name="sis01", tag="values3")
+        sis = [sis01[:, 0, :], sis01[:, 1, :]]
         for c in range(2):
-            nc.vector.tensor_copy(sis[c][:], page[c][:].indirect(idx4[:]))
+            nc.vector.tensor_copy(sis[c], page[c][:].indirect(idx4[:]))
 
         x_codes = [keep.tile([P, N], U32, name=f"x_codes{b}", align_bytes=64) for b in range(PICKS // N)]
         x_sc = [keep.tile([P, N], U8, name=f"x_sc{b}", align_bytes=64) for b in range(PICKS // N)]
@@ -258,11 +263,10 @@ def tile_list_cask_blend_scores_kernel(tc, tab_words, tab_scales, offs, w1_words
                                 rhs=x_codes[b][:].bitcast(FP8X4), rhs_scale=x_sc[b][:], start=True, stop=True)
             res = ring.tile([P, N], F32, name="res", bufs=8)
             if i < on_gpsimd:
-                y_sb = ring.tile([P, N], F32, name="y_sb", bufs=5)
-                nc.scalar.copy(y_sb[:], y[:])
+                nc.scalar.copy(res[:], y[:])
                 scaled = ring.tile([P, N], F32, name="scaled", bufs=5)
                 nc.scalar.activation(scaled[:], sis[c][:, entries], ACT.Copy, scale=neg_sister[:, c:c + 1])
-                nc.gpsimd.tensor_tensor(res[:], y_sb[:], scaled[:], ALU.add)
+                nc.gpsimd.tensor_tensor(res[:], res[:], scaled[:], ALU.add)
             else:
                 nc.vector.scalar_tensor_tensor(res[:], sis[c][:, entries], neg_sister[:, c:c + 1], y[:], ALU.mult, ALU.add)
             nc.sync.dma_start(out[c * P:(c + 1) * P, entries], res[:])

@@ -23,7 +23,12 @@ PASSES = K // (P * PACK)
 SLICES = H // P
 N = 512
 QUADS = 4
-BLOCKS = N // P
+TURNS = N // P
+GROUP = 16
+FIRST = N // 2
+TURN_BANKS = 4
+GPSIMD_PIECES = [(0, 0), (1, 0), (2, 0), (0, 1)]
+VECTOR_PIECES = [(3, 0), (1, 1), (2, 1), (3, 1)]
 
 
 def tile_list_cask_blend_scores_kernel(tc, tab_words, tab_scales, offs, w1_words, w1_scales, w2, gain, page0,
@@ -34,15 +39,16 @@ def tile_list_cask_blend_scores_kernel(tc, tab_words, tab_scales, offs, w1_words
         ring = ctx.enter_context(tc.tile_pool(name="ring", bufs=2))
         psum = ctx.enter_context(tc.psum_pool(name="psum", bufs=2))
         halves = [slice(b * N, (b + 1) * N) for b in range(S // N)]
+        first, second, later = slice(0, FIRST), slice(FIRST, N), slice(FIRST, S)
 
         def load_list(src, name):
-            lst = keep.tile([P, S // 16], U16, name=name)
+            lst = keep.tile([P, S // GROUP], U16, name=name)
             nc.sync.dma_start(lst[:], src)
             return lst
 
         def load_channel_vector(src, name):
             vec = keep.tile([P, SLICES], F32, name=name)
-            with nc.allow_non_contiguous_dma(reason="one value for each channel and partition"):
+            with nc.allow_non_contiguous_dma(reason="one value for each slice and partition"):
                 nc.sync.dma_start(vec[:], src.rearrange("(c p) -> p c", p=P))
             return vec
 
@@ -54,7 +60,7 @@ def tile_list_cask_blend_scores_kernel(tc, tab_words, tab_scales, offs, w1_words
             return [raw[:, :, :, (c - c0) * P:(c - c0 + 1) * P] for c in range(c0, c1)]
 
         def columns(lst, entries):
-            return lst[:, entries.start // 16:entries.stop // 16]
+            return lst[:, entries.start // GROUP:entries.stop // GROUP]
 
         tab_sc = keep.tile([P, T], U8, name="tab_sc")
         nc.vector.memset(tab_sc[32:64].bitcast(I32), 0)
@@ -84,7 +90,6 @@ def tile_list_cask_blend_scores_kernel(tc, tab_words, tab_scales, offs, w1_words
         gain_sb = load_channel_vector(gain, "gain_sb")
         idx2 = load_list(offs2, "idx2")
         wgs_sb = keep.tile([P, S], F32, name="wgs_sb")
-        first, later = slice(0, N // 2), slice(N // 2, S)
         nc.sync.dma_start(wgs_sb[:, first], wgs[:, first])
         w2_raw = w2_raw + load_w2(1, 2)
         nc.sync.dma_start(wgs_sb[:, later], wgs[:, later])
@@ -101,10 +106,6 @@ def tile_list_cask_blend_scores_kernel(tc, tab_words, tab_scales, offs, w1_words
         for q in range(QUADS):
             nc.sync.dma_start(w3_sc[32 * q:32 * q + 4].bitcast(I32), w3_scales[0, 4 * q:4 * q + 4, :].bitcast(I32))
 
-        warm = keep.tile([P, 1], F32, name="warm")
-        warm_in = keep.tile([P, 1], F32, name="warm_in")
-        nc.gpsimd.memset(warm_in[:], 0.0)
-        nc.scalar.activation(warm[:], warm_in[:], ACT.Abs_reciprocal_sqrt, bias=1.0)
         ident_bf = keep.tile([P, P], BF16, name="ident_bf")
         make_identity(nc, ident_bf[:])
         ident_f32 = keep.tile([P, P], F32, name="ident_f32")
@@ -114,7 +115,7 @@ def tile_list_cask_blend_scores_kernel(tc, tab_words, tab_scales, offs, w1_words
         w2_sc = [keep.tile([P, PASSES, P], U8, name=f"w2_sc{c}", align_bytes=64) for c in range(SLICES)]
 
         def quantise_w2(c, copy):
-            grouped = keep.tile([P, PASSES, P, PACK], BF16, name=f"w2_bf{c}", tag=f"chain{c}", align_bytes=64)
+            grouped = keep.tile([P, PASSES, P, PACK], BF16, name=f"w2_bf{c}", tag=f"after_w2_{c}", align_bytes=64)
             for a in range(PASSES):
                 copy(grouped[:, a].rearrange("p (m e) i -> p m i e", e=4),
                      w2_raw[c][:, a].rearrange("p i (m e) -> p m i e", e=4))
@@ -141,93 +142,105 @@ def tile_list_cask_blend_scores_kernel(tc, tab_words, tab_scales, offs, w1_words
                                     start=(a == 0), stop=(a == PASSES - 1))
 
         def lead_of(c, entries):
-            lead = psum.tile([P, N], F32, name="lead", tag="acc0")
+            lead = psum.tile([P, N], F32, name="lead", tag="lead")
             accumulate(lead[:], [w1_codes[:, a, 2 * P * c:2 * P * (c + 1)].bitcast(FP4X4) for a in range(PASSES)],
                        [w1_sc[:, a, P * c:P * (c + 1)] for a in range(PASSES)], entries)
             return lead
 
         def damp_of(c, entries, damp):
             width = entries.stop - entries.start
-            temper = psum.tile([P, width], F32, name="temper", tag="acc1")
+            temper = psum.tile([P, width], F32, name="temper", tag="temper")
             accumulate(temper[:], [w2_codes[c][:, a].bitcast(FP8X4) for a in range(PASSES)],
                        [w2_sc[c][:, a] for a in range(PASSES)], entries)
             sq = ring.tile([P, width], F32, name="sq")
             nc.scalar.activation(sq[:], temper[:], ACT.Square)
             nc.scalar.activation(damp, sq[:], ACT.Abs_reciprocal_sqrt, bias=1.0)
 
-        x_rows = [keep.tile([P, BLOCKS, H], BF16, name=f"x_rows{b}") for b in range(PICKS // N)]
+        x_rows = [keep.tile([P, TURNS, H], BF16, name=f"x_rows{b}") for b in range(PICKS // N)]
 
         def reread_casks(c, entries, picked):
             nc.vector.tensor_copy(picked, page[c][:].indirect(columns(idx3, entries)))
             for e0 in range(0, entries.stop - entries.start, N):
                 x_c = ring.tile([P, N], BF16, name="x_c")
                 nc.scalar.activation(x_c[:], picked[:, e0:e0 + N], ACT.Copy, scale=reread_sb[:, c:c + 1])
-                turned = psum.tile([P, BLOCKS, P], BF16, name="turned", tag="turn", bufs=4)
-                for jb in range(BLOCKS):
+                turned = psum.tile([P, TURNS, P], BF16, name="turned", tag="turn", bufs=TURN_BANKS)
+                for jb in range(TURNS):
                     nc.tensor.transpose(turned[:, jb, :], x_c[:, jb * P:(jb + 1) * P], ident_bf[:])
                 nc.scalar.copy(x_rows[(entries.start + e0) // N][:, :, c * P:(c + 1) * P], turned[:])
 
-        def first_damp(entries):
-            damp = ring.tile([P, entries.stop - entries.start], F32, name="damp_first", bufs=3)
+        def damp_piece(entries):
+            damp = ring.tile([P, entries.stop - entries.start], F32, name="damp_piece", bufs=3)
             damp_of(0, entries, damp[:])
             return damp
 
-        def features(h, lead, factor):
-            nc.vector.scalar_tensor_tensor(h, lead, gain_sb[:, 0:1], factor, ALU.mult, ALU.mult)
+        def gained_times(c, product, lead, factor):
+            nc.vector.scalar_tensor_tensor(product, lead, gain_sb[:, c:c + 1], factor, ALU.mult, ALU.mult)
 
         def scatter(c, entries, values):
             nc.vector.tensor_copy(page[c][:].indirect(columns(idx2, entries)), values)
 
-        second = slice(N // 2, N)
-        damps = [first_damp(first)]
+        damps = [damp_piece(first)]
         leads = [lead_of(0, halves[0])]
-        damps.append(first_damp(second))
-        damps.append(first_damp(halves[1]))
+        damps.append(damp_piece(second))
+        damps.append(damp_piece(halves[1]))
         leads.append(lead_of(0, halves[1]))
-        h_first = keep.tile([P, N // 2], F32, name="h_first")
-        features(h_first[:], leads[0][:, first], damps[0][:])
+        h_first = keep.tile([P, FIRST], F32, name="h_first")
+        gained_times(0, h_first[:], leads[0][:, first], damps[0][:])
         nc.vector.tensor_tensor(page[0][:].indirect(columns(idx2, first)), h_first[:], wgs_sb[:, first], ALU.mult)
-        weight = keep.tile([P, S - N // 2], F32, name="weight0")
-        nc.gpsimd.tensor_tensor(weight[:, 0:N // 2], damps[1][:], wgs_sb[:, second], ALU.mult)
-        nc.gpsimd.tensor_tensor(weight[:, N // 2:], damps[2][:], wgs_sb[:, halves[1]], ALU.mult)
         quantise_w2(1, nc.scalar.copy)
-        h_later = keep.tile([P, S - N // 2], F32, name="h_later", tag="chain1", align_bytes=64)
-        features(h_later[:, 0:N // 2], leads[0][:, second], weight[:, 0:N // 2])
-        features(h_later[:, N // 2:], leads[1][:], weight[:, N // 2:])
-        scatter(0, later, h_later[:])
+        h_later = keep.tile([P, S - FIRST], F32, name="h_later", tag="after_w2_1", align_bytes=64)
+        gained_times(0, h_later[:, 0:N - FIRST], leads[0][:, second], damps[1][:])
+        gained_times(0, h_later[:, N - FIRST:], leads[1][:], damps[2][:])
+        values = keep.tile([P, S - FIRST], F32, name="values0")
+        nc.vector.tensor_tensor(values[:, 0:N - FIRST], h_later[:, 0:N - FIRST], wgs_sb[:, second], ALU.mult)
+        nc.vector.tensor_tensor(values[:, N - FIRST:], h_later[:, N - FIRST:], wgs_sb[:, halves[1]], ALU.mult)
+        scatter(0, later, values[:])
 
         damp = {c: keep.tile([P, S], F32, name=f"damp{c}") for c in range(1, SLICES)}
-        gained = {c: keep.tile([P, S], F32, name=f"gained{c}", tag=f"gained{c}") for c in range(1, SLICES)}
 
-        def factors(c):
+        def damp_slice(c):
             for entries in halves:
                 damp_of(c, entries, damp[c][:, entries])
+
+        def gained_slice(c):
+            gained = keep.tile([P, S], F32, name=f"gained{c}")
+            for entries in halves:
                 lead = lead_of(c, entries)
-                nc.scalar.activation(gained[c][:, entries], lead[:], ACT.Copy, scale=gain_sb[:, c:c + 1])
+                nc.scalar.activation(gained[:, entries], lead[:], ACT.Copy, scale=gain_sb[:, c:c + 1])
+            return gained
+
+        def weight_of(c, entries):
+            weight = ring.tile([P, N], F32, name="weight")
+            nc.gpsimd.tensor_tensor(weight[:], damp[c][:, entries], wgs_sb[:, entries], ALU.mult)
+            return weight
+
+        def reread_whole(c):
+            picked = keep.tile([P, PICKS], F32, name=f"picked{c}", tag=f"after_w2_{c + 2}", align_bytes=64)
+            reread_casks(c, slice(0, PICKS), picked[:])
 
         quantise_w2(2, nc.scalar.copy)
-        factors(1)
+        damp_slice(1)
         quantise_w2(3, nc.scalar.copy)
-        factors(2)
-        picked = keep.tile([P, PICKS], F32, name="picked0", tag="chain2", align_bytes=64)
-        reread_casks(0, slice(0, PICKS), picked[:])
-        factors(3)
-        for c in range(1, SLICES):
-            values = keep.tile([P, S], F32, name=f"values{c}", tag=f"values{c}")
+        damp_slice(2)
+        reread_whole(0)
+        values = keep.tile([P, S], F32, name="values1")
+        for entries in halves:
+            gained_times(1, values[:, entries], lead_of(1, entries)[:], weight_of(1, entries)[:])
+        scatter(1, slice(0, S), values[:])
+        gained = {2: gained_slice(2)}
+        damp_slice(3)
+        gained[3] = gained_slice(3)
+        for c in range(2, SLICES):
+            reread_whole(c - 1)
+            values = keep.tile([P, S], F32, name=f"values{c}", tag=f"after_scatter_{c}")
             for entries in halves:
-                weight = ring.tile([P, N], F32, name="weight")
-                nc.gpsimd.tensor_tensor(weight[:], damp[c][:, entries], wgs_sb[:, entries], ALU.mult)
-                nc.gpsimd.tensor_tensor(values[:, entries], gained[c][:, entries], weight[:], ALU.mult)
+                nc.gpsimd.tensor_tensor(values[:, entries], gained[c][:, entries], weight_of(c, entries)[:], ALU.mult)
             scatter(c, slice(0, S), values[:])
-            if c < SLICES - 1:
-                picked = keep.tile([P, PICKS], F32, name=f"picked{c}", tag=f"chain{c + 2}", align_bytes=64)
-                reread_casks(c, slice(0, PICKS), picked[:])
-            else:
-                for entries in halves:
-                    picked = ring.tile([P, N], F32, name="picked_last")
-                    reread_casks(c, entries, picked[:])
+        for entries in halves:
+            picked = ring.tile([P, N], F32, name="picked_last")
+            reread_casks(SLICES - 1, entries, picked[:])
 
-        sis01 = keep.tile([P, 2, PICKS], F32, name="sis01", tag="values3")
+        sis01 = keep.tile([P, 2, PICKS], F32, name="sis01", tag=f"after_scatter_{SLICES - 1}")
         sis = [sis01[:, 0, :], sis01[:, 1, :]]
         for c in range(2):
             nc.vector.tensor_copy(sis[c], page[c][:].indirect(idx4[:]))
@@ -235,10 +248,10 @@ def tile_list_cask_blend_scores_kernel(tc, tab_words, tab_scales, offs, w1_words
         x_codes = [keep.tile([P, N], U32, name=f"x_codes{b}", align_bytes=64) for b in range(PICKS // N)]
         x_sc = [keep.tile([P, N], U8, name=f"x_sc{b}", align_bytes=64) for b in range(PICKS // N)]
         for b in range(PICKS // N):
-            x_grouped = keep.tile([P, N, PACK], BF16, name=f"x_grouped{b}", tag=f"x_grouped{b}", align_bytes=64)
+            x_grouped = keep.tile([P, N, PACK], BF16, name=f"x_grouped{b}", tag=f"after_x_{b}", align_bytes=64)
             words = x_rows[b][:].bitcast(F32)
-            for j0 in range(0, BLOCKS, 2):
-                back = psum.tile([P, 2, 2, P], F32, name="back", tag="turn", bufs=4)
+            for j0 in range(0, TURNS, 2):
+                back = psum.tile([P, 2, 2, P], F32, name="back", tag="turn", bufs=TURN_BANKS)
                 for jb in range(2):
                     for u in range(2):
                         nc.tensor.transpose(back[:, jb, u, :], words[:, j0 + jb, u::2], ident_f32[:])
@@ -247,26 +260,28 @@ def tile_list_cask_blend_scores_kernel(tc, tab_words, tab_scales, offs, w1_words
             nc.vector.quantize_mx(out=x_codes[b][:].bitcast(FP8X4), scales=x_sc[b][:],
                                   in_=x_grouped[:].rearrange("p j t -> p (j t)"))
         for c in range(2, SLICES):
-            sis.append(keep.tile([P, PICKS], F32, name=f"sis{c}", tag=f"x_grouped{c - 2}", align_bytes=64))
-            nc.vector.tensor_copy(sis[c][:], page[c][:].indirect(idx4[:]))
+            sis_late = keep.tile([P, PICKS], F32, name=f"sis{c}", tag=f"after_x_{c - 2}", align_bytes=64)
+            sis.append(sis_late[:])
+            nc.vector.tensor_copy(sis[c], page[c][:].indirect(idx4[:]))
 
-        pieces = [(0, 0), (1, 0), (2, 0), (0, 1), (1, 1), (3, 0), (2, 1), (3, 1)]
-        on_gpsimd = 5
-        for i, (c, b) in enumerate(pieces):
-            entries = halves[b]
-            if i < 4:
-                y = psum.tile([P, N], F32, name="y", tag=f"acc{i % 2}")
-            else:
-                y = psum.tile([P, N], F32, name="y", tag="turn", bufs=4)
-            nc.tensor.matmul_mx(out=y[:], lhsT=w3_codes[:, P * c:P * (c + 1)].bitcast(FP8X4),
+        def product(y, c, b):
+            nc.tensor.matmul_mx(out=y, lhsT=w3_codes[:, P * c:P * (c + 1)].bitcast(FP8X4),
                                 lhsT_scale=w3_sc[:, P * c:P * (c + 1)],
                                 rhs=x_codes[b][:].bitcast(FP8X4), rhs_scale=x_sc[b][:], start=True, stop=True)
-            res = ring.tile([P, N], F32, name="res", bufs=8)
-            if i < on_gpsimd:
-                nc.scalar.copy(res[:], y[:])
-                scaled = ring.tile([P, N], F32, name="scaled", bufs=5)
-                nc.scalar.activation(scaled[:], sis[c][:, entries], ACT.Copy, scale=neg_sister[:, c:c + 1])
-                nc.gpsimd.tensor_tensor(res[:], res[:], scaled[:], ALU.add)
-            else:
-                nc.vector.scalar_tensor_tensor(res[:], sis[c][:, entries], neg_sister[:, c:c + 1], y[:], ALU.mult, ALU.add)
-            nc.sync.dma_start(out[c * P:(c + 1) * P, entries], res[:])
+
+        pieces = len(GPSIMD_PIECES) + len(VECTOR_PIECES)
+        for i, (c, b) in enumerate(GPSIMD_PIECES):
+            y = psum.tile([P, N], F32, name="y", tag=("lead", "temper")[i % 2])
+            product(y[:], c, b)
+            res = ring.tile([P, N], F32, name="res", bufs=pieces)
+            nc.scalar.copy(res[:], y[:])
+            scaled = ring.tile([P, N], F32, name="scaled", bufs=len(GPSIMD_PIECES))
+            nc.scalar.activation(scaled[:], sis[c][:, halves[b]], ACT.Copy, scale=neg_sister[:, c:c + 1])
+            nc.gpsimd.tensor_tensor(res[:], res[:], scaled[:], ALU.add)
+            nc.sync.dma_start(out[c * P:(c + 1) * P, halves[b]], res[:])
+        for c, b in VECTOR_PIECES:
+            y = psum.tile([P, N], F32, name="y", tag="turn", bufs=TURN_BANKS)
+            product(y[:], c, b)
+            res = ring.tile([P, N], F32, name="res", bufs=pieces)
+            nc.vector.scalar_tensor_tensor(res[:], sis[c][:, halves[b]], neg_sister[:, c:c + 1], y[:], ALU.mult, ALU.add)
+            nc.sync.dma_start(out[c * P:(c + 1) * P, halves[b]], res[:])

from contextlib import ExitStack

import concourse.mybir as mybir
from concourse.masks import make_identity

K, T, S, H, T2, PICKS = 1024, 4096, 1024, 512, 2048, 1024
FLOPS = 2 * (2 * K * H * S + H * H * PICKS)

F32 = mybir.dt.float32
BF16 = mybir.dt.bfloat16
I32 = mybir.dt.int32
U32 = mybir.dt.uint32
U16 = mybir.dt.uint16
U8 = mybir.dt.uint8
FP8X4 = mybir.dt.float8_e4m3fn_x4
FP4X4 = mybir.dt.float4_e2m1fn_x4
ALU = mybir.AluOpType
ACT = mybir.ActivationFunctionType

P = 128
PACK = 4
PASSES = K // (P * PACK)
SLICES = H // P
N = 512
QUADS = 4
TURNS = N // P
GROUP = 16
FIRST = N // 2
TURN_BANKS = 4
GPSIMD_PIECES = [(0, 0), (1, 0), (2, 0), (0, 1)]
VECTOR_PIECES = [(3, 0), (1, 1), (2, 1), (3, 1)]


def tile_list_cask_blend_scores_kernel(tc, tab_words, tab_scales, offs, w1_words, w1_scales, w2, gain, page0,
                                                wgs, offs2, offs3, offs4, reread, w3_words, w3_scales, sister, out):
    nc = tc.nc
    with ExitStack() as ctx:
        keep = ctx.enter_context(tc.tile_pool(name="keep", bufs=1))
        ring = ctx.enter_context(tc.tile_pool(name="ring", bufs=2))
        psum = ctx.enter_context(tc.psum_pool(name="psum", bufs=2))
        halves = [slice(b * N, (b + 1) * N) for b in range(S // N)]
        first, second, later = slice(0, FIRST), slice(FIRST, N), slice(FIRST, S)

        def load_list(src, name):
            lst = keep.tile([P, S // GROUP], U16, name=name)
            nc.sync.dma_start(lst[:], src)
            return lst

        def load_channel_vector(src, name):
            vec = keep.tile([P, SLICES], F32, name=name)
            with nc.allow_non_contiguous_dma(reason="one value for each slice and partition"):
                nc.sync.dma_start(vec[:], src.rearrange("(c p) -> p c", p=P))
            return vec

        def load_w2(c0, c1):
            raw = keep.tile([P, PASSES, PACK, (c1 - c0) * P], F32, name=f"w2_raw{c0}")
            for a in range(PASSES):
                rows = w2[a * P * PACK:(a + 1) * P * PACK, c0 * P:c1 * P]
                nc.sync.dma_start(raw[:, a], rows.rearrange("(p i) m -> p i m", i=PACK))
            return [raw[:, :, :, (c - c0) * P:(c - c0 + 1) * P] for c in range(c0, c1)]

        def columns(lst, entries):
            return lst[:, entries.start // GROUP:entries.stop // GROUP]

        tab_sc = keep.tile([P, T], U8, name="tab_sc")
        nc.vector.memset(tab_sc[32:64].bitcast(I32), 0)
        nc.vector.memset(tab_sc[64:128].bitcast(I32), 0)

        idx = load_list(offs, "idx")
        nc.sync.dma_start(tab_sc[0:32].bitcast(I32), tab_scales.rearrange("a q t -> q a t").bitcast(I32))
        tab = [keep.tile([P, T], I32, name=f"tab{a}") for a in range(PASSES)]
        nc.sync.dma_start(tab[0][:], tab_words[0].rearrange("p t i -> p (t i)").bitcast(I32))
        w1_sc = keep.tile([P, PASSES, H], U8, name="w1_sc", align_bytes=64)
        for q in range(QUADS):
            nc.sync.dma_start(w1_sc[32 * q:32 * q + 4].bitcast(I32),
                              w1_scales[:, 4 * q:4 * q + 4, :].rearrange("a r c -> r a c").bitcast(I32))
        w2_raw = load_w2(0, 1)
        nc.sync.dma_start(tab[1][:], tab_words[1].rearrange("p t i -> p (t i)").bitcast(I32))

        v_sc_rows = keep.tile([P, S], U8, name="v_sc_rows")
        nc.vector.tensor_copy(v_sc_rows[:], tab_sc[:].indirect(idx[:]))
        v_sc = keep.tile([P, PASSES, S], U8, name="v_sc", align_bytes=64)
        for q in range(QUADS):
            nc.sync.dma_start(v_sc[32 * q:32 * q + 4].bitcast(I32), v_sc_rows[8 * q:8 * q + 8].bitcast(I32))

        w1_codes = keep.tile([P, PASSES, 2 * H], U8, name="w1_codes", align_bytes=64)
        nc.sync.dma_start(w1_codes[:].bitcast(I32), w1_words.rearrange("a p c -> p a c").bitcast(I32))
        page = [keep.tile([P, T2], F32, name=f"page{c}") for c in range(SLICES)]
        nc.sync.dma_start(page[0][:], page0[0:P, :])
        gain_sb = load_channel_vector(gain, "gain_sb")
        idx2 = load_list(offs2, "idx2")
        wgs_sb = keep.tile([P, S], F32, name="wgs_sb")
        nc.sync.dma_start(wgs_sb[:, first], wgs[:, first])
        w2_raw = w2_raw + load_w2(1, 2)
        nc.sync.dma_start(wgs_sb[:, later], wgs[:, later])
        w2_raw = w2_raw + load_w2(2, SLICES)
        idx3 = load_list(offs3, "idx3")
        reread_sb = load_channel_vector(reread, "reread_sb")
        for c in range(1, SLICES):
            nc.sync.dma_start(page[c][:], page0[c * P:(c + 1) * P, :])
        idx4 = load_list(offs4, "idx4")
        sister_sb = load_channel_vector(sister, "sister_sb")
        w3_codes = keep.tile([P, H], I32, name="w3_codes", align_bytes=64)
        nc.sync.dma_start(w3_codes[:], w3_words[0].rearrange("p c i -> p (c i)").bitcast(I32))
        w3_sc = keep.tile([P, H], U8, name="w3_sc", align_bytes=64)
        for q in range(QUADS):
            nc.sync.dma_start(w3_sc[32 * q:32 * q + 4].bitcast(I32), w3_scales[0, 4 * q:4 * q + 4, :].bitcast(I32))

        ident_bf = keep.tile([P, P], BF16, name="ident_bf")
        make_identity(nc, ident_bf[:])
        ident_f32 = keep.tile([P, P], F32, name="ident_f32")
        make_identity(nc, ident_f32[:])

        w2_codes = [keep.tile([P, PASSES, P], U32, name=f"w2_codes{c}", align_bytes=64) for c in range(SLICES)]
        w2_sc = [keep.tile([P, PASSES, P], U8, name=f"w2_sc{c}", align_bytes=64) for c in range(SLICES)]

        def quantise_w2(c, copy):
            grouped = keep.tile([P, PASSES, P, PACK], BF16, name=f"w2_bf{c}", tag=f"after_w2_{c}", align_bytes=64)
            for a in range(PASSES):
                copy(grouped[:, a].rearrange("p (m e) i -> p m i e", e=4),
                     w2_raw[c][:, a].rearrange("p i (m e) -> p m i e", e=4))
            nc.vector.quantize_mx(out=w2_codes[c][:].rearrange("p a m -> p (a m)").bitcast(FP8X4),
                                  scales=w2_sc[c][:].rearrange("p a m -> p (a m)"),
                                  in_=grouped[:].rearrange("p a m i -> p (a m i)"))

        v = [[keep.tile([P, N], U32, name=f"v{a}{b}", align_bytes=64) for b in range(S // N)] for a in range(PASSES)]
        for b, entries in enumerate(halves):
            nc.vector.tensor_copy(v[0][b][:], tab[0][:].bitcast(U32).indirect(columns(idx, entries)))
        quantise_w2(0, nc.vector.tensor_copy)
        for b, entries in enumerate(halves):
            nc.vector.tensor_copy(v[1][b][:], tab[1][:].bitcast(U32).indirect(columns(idx, entries)))

        neg_sister = keep.tile([P, SLICES], F32, name="neg_sister")
        nc.scalar.mul(neg_sister[:], sister_sb[:], -1.0)

        def accumulate(acc, codes, scales, entries):
            b, c0 = divmod(entries.start, N)
            part = slice(c0, c0 + entries.stop - entries.start)
            for a in range(PASSES):
                nc.tensor.matmul_mx(out=acc, lhsT=codes[a], lhsT_scale=scales[a],
                                    rhs=v[a][b][:, part].bitcast(FP8X4), rhs_scale=v_sc[:, a, entries],
                                    start=(a == 0), stop=(a == PASSES - 1))

        def lead_of(c, entries):
            lead = psum.tile([P, N], F32, name="lead", tag="lead")
            accumulate(lead[:], [w1_codes[:, a, 2 * P * c:2 * P * (c + 1)].bitcast(FP4X4) for a in range(PASSES)],
                       [w1_sc[:, a, P * c:P * (c + 1)] for a in range(PASSES)], entries)
            return lead

        def damp_of(c, entries, damp):
            width = entries.stop - entries.start
            temper = psum.tile([P, width], F32, name="temper", tag="temper")
            accumulate(temper[:], [w2_codes[c][:, a].bitcast(FP8X4) for a in range(PASSES)],
                       [w2_sc[c][:, a] for a in range(PASSES)], entries)
            sq = ring.tile([P, width], F32, name="sq")
            nc.scalar.activation(sq[:], temper[:], ACT.Square)
            nc.scalar.activation(damp, sq[:], ACT.Abs_reciprocal_sqrt, bias=1.0)

        x_rows = [keep.tile([P, TURNS, H], BF16, name=f"x_rows{b}") for b in range(PICKS // N)]

        def reread_casks(c, entries, picked):
            nc.vector.tensor_copy(picked, page[c][:].indirect(columns(idx3, entries)))
            for e0 in range(0, entries.stop - entries.start, N):
                x_c = ring.tile([P, N], BF16, name="x_c")
                nc.scalar.activation(x_c[:], picked[:, e0:e0 + N], ACT.Copy, scale=reread_sb[:, c:c + 1])
                turned = psum.tile([P, TURNS, P], BF16, name="turned", tag="turn", bufs=TURN_BANKS)
                for jb in range(TURNS):
                    nc.tensor.transpose(turned[:, jb, :], x_c[:, jb * P:(jb + 1) * P], ident_bf[:])
                nc.scalar.copy(x_rows[(entries.start + e0) // N][:, :, c * P:(c + 1) * P], turned[:])

        def damp_piece(entries):
            damp = ring.tile([P, entries.stop - entries.start], F32, name="damp_piece", bufs=3)
            damp_of(0, entries, damp[:])
            return damp

        def gained_times(c, product, lead, factor):
            nc.vector.scalar_tensor_tensor(product, lead, gain_sb[:, c:c + 1], factor, ALU.mult, ALU.mult)

        def scatter(c, entries, values):
            nc.vector.tensor_copy(page[c][:].indirect(columns(idx2, entries)), values)

        damps = [damp_piece(first)]
        leads = [lead_of(0, halves[0])]
        damps.append(damp_piece(second))
        damps.append(damp_piece(halves[1]))
        leads.append(lead_of(0, halves[1]))
        h_first = keep.tile([P, FIRST], F32, name="h_first")
        gained_times(0, h_first[:], leads[0][:, first], damps[0][:])
        nc.vector.tensor_tensor(page[0][:].indirect(columns(idx2, first)), h_first[:], wgs_sb[:, first], ALU.mult)
        quantise_w2(1, nc.scalar.copy)
        h_later = keep.tile([P, S - FIRST], F32, name="h_later", tag="after_w2_1", align_bytes=64)
        gained_times(0, h_later[:, 0:N - FIRST], leads[0][:, second], damps[1][:])
        gained_times(0, h_later[:, N - FIRST:], leads[1][:], damps[2][:])
        values = keep.tile([P, S - FIRST], F32, name="values0")
        nc.vector.tensor_tensor(values[:, 0:N - FIRST], h_later[:, 0:N - FIRST], wgs_sb[:, second], ALU.mult)
        nc.vector.tensor_tensor(values[:, N - FIRST:], h_later[:, N - FIRST:], wgs_sb[:, halves[1]], ALU.mult)
        scatter(0, later, values[:])

        damp = {c: keep.tile([P, S], F32, name=f"damp{c}") for c in range(1, SLICES)}

        def damp_slice(c):
            for entries in halves:
                damp_of(c, entries, damp[c][:, entries])

        def gained_slice(c):
            gained = keep.tile([P, S], F32, name=f"gained{c}")
            for entries in halves:
                lead = lead_of(c, entries)
                nc.scalar.activation(gained[:, entries], lead[:], ACT.Copy, scale=gain_sb[:, c:c + 1])
            return gained

        def weight_of(c, entries):
            weight = ring.tile([P, N], F32, name="weight")
            nc.gpsimd.tensor_tensor(weight[:], damp[c][:, entries], wgs_sb[:, entries], ALU.mult)
            return weight

        def reread_whole(c):
            picked = keep.tile([P, PICKS], F32, name=f"picked{c}", tag=f"after_w2_{c + 2}", align_bytes=64)
            reread_casks(c, slice(0, PICKS), picked[:])

        quantise_w2(2, nc.scalar.copy)
        damp_slice(1)
        quantise_w2(3, nc.scalar.copy)
        damp_slice(2)
        reread_whole(0)
        values = keep.tile([P, S], F32, name="values1")
        for entries in halves:
            gained_times(1, values[:, entries], lead_of(1, entries)[:], weight_of(1, entries)[:])
        scatter(1, slice(0, S), values[:])
        gained = {2: gained_slice(2)}
        damp_slice(3)
        gained[3] = gained_slice(3)
        for c in range(2, SLICES):
            reread_whole(c - 1)
            values = keep.tile([P, S], F32, name=f"values{c}", tag=f"after_scatter_{c}")
            for entries in halves:
                nc.gpsimd.tensor_tensor(values[:, entries], gained[c][:, entries], weight_of(c, entries)[:], ALU.mult)
            scatter(c, slice(0, S), values[:])
        for entries in halves:
            picked = ring.tile([P, N], F32, name="picked_last")
            reread_casks(SLICES - 1, entries, picked[:])

        sis01 = keep.tile([P, 2, PICKS], F32, name="sis01", tag=f"after_scatter_{SLICES - 1}")
        sis = [sis01[:, 0, :], sis01[:, 1, :]]
        for c in range(2):
            nc.vector.tensor_copy(sis[c], page[c][:].indirect(idx4[:]))

        x_codes = [keep.tile([P, N], U32, name=f"x_codes{b}", align_bytes=64) for b in range(PICKS // N)]
        x_sc = [keep.tile([P, N], U8, name=f"x_sc{b}", align_bytes=64) for b in range(PICKS // N)]
        for b in range(PICKS // N):
            x_grouped = keep.tile([P, N, PACK], BF16, name=f"x_grouped{b}", tag=f"after_x_{b}", align_bytes=64)
            words = x_rows[b][:].bitcast(F32)
            for j0 in range(0, TURNS, 2):
                back = psum.tile([P, 2, 2, P], F32, name="back", tag="turn", bufs=TURN_BANKS)
                for jb in range(2):
                    for u in range(2):
                        nc.tensor.transpose(back[:, jb, u, :], words[:, j0 + jb, u::2], ident_f32[:])
                nc.scalar.copy(x_grouped[:, j0 * P:(j0 + 2) * P, :].bitcast(F32).rearrange("p (jb j) u -> p jb j u", jb=2),
                               back[:].rearrange("p jb u j -> p jb j u"))
            nc.vector.quantize_mx(out=x_codes[b][:].bitcast(FP8X4), scales=x_sc[b][:],
                                  in_=x_grouped[:].rearrange("p j t -> p (j t)"))
        for c in range(2, SLICES):
            sis_late = keep.tile([P, PICKS], F32, name=f"sis{c}", tag=f"after_x_{c - 2}", align_bytes=64)
            sis.append(sis_late[:])
            nc.vector.tensor_copy(sis[c], page[c][:].indirect(idx4[:]))

        def product(y, c, b):
            nc.tensor.matmul_mx(out=y, lhsT=w3_codes[:, P * c:P * (c + 1)].bitcast(FP8X4),
                                lhsT_scale=w3_sc[:, P * c:P * (c + 1)],
                                rhs=x_codes[b][:].bitcast(FP8X4), rhs_scale=x_sc[b][:], start=True, stop=True)

        pieces = len(GPSIMD_PIECES) + len(VECTOR_PIECES)
        for i, (c, b) in enumerate(GPSIMD_PIECES):
            y = psum.tile([P, N], F32, name="y", tag=("lead", "temper")[i % 2])
            product(y[:], c, b)
            res = ring.tile([P, N], F32, name="res", bufs=pieces)
            nc.scalar.copy(res[:], y[:])
            scaled = ring.tile([P, N], F32, name="scaled", bufs=len(GPSIMD_PIECES))
            nc.scalar.activation(scaled[:], sis[c][:, halves[b]], ACT.Copy, scale=neg_sister[:, c:c + 1])
            nc.gpsimd.tensor_tensor(res[:], res[:], scaled[:], ALU.add)
            nc.sync.dma_start(out[c * P:(c + 1) * P, halves[b]], res[:])
        for c, b in VECTOR_PIECES:
            y = psum.tile([P, N], F32, name="y", tag="turn", bufs=TURN_BANKS)
            product(y[:], c, b)
            res = ring.tile([P, N], F32, name="res", bufs=pieces)
            nc.vector.scalar_tensor_tensor(res[:], sis[c][:, halves[b]], neg_sister[:, c:c + 1], y[:], ALU.mult, ALU.add)
            nc.sync.dma_start(out[c * P:(c + 1) * P, halves[b]], res[:])
